import numpy as np
import ml_dtypes


def mxq(x, axis, fmt="e4m3"):
    dtype, down = {"e4m3": (ml_dtypes.float8_e4m3fn, 7), "e5m2": (ml_dtypes.float8_e5m2, 14)}[fmt]
    v = np.moveaxis(np.asarray(x, np.float32).astype(ml_dtypes.bfloat16).astype(np.float64), axis, -1)
    blocks = v.reshape(v.shape[:-1] + (-1, 32))
    amax = np.abs(blocks).max(-1, keepdims=True)
    byte = np.maximum(np.where(amax > 0, np.frexp(amax)[1] - 1 + 127, 0) - down, 1)
    scale = np.exp2(byte - 127.0)
    codes = (blocks / scale).astype(np.float32).astype(dtype).astype(np.float64)
    return np.moveaxis((codes * scale).reshape(v.shape), -1, axis)


WIDE = False


def mx_kscale(k):
    if not WIDE:
        return np.ones(k)
    levels = np.array([10, -10, 5, -5, 0])
    if k % 512:
        return np.exp2(np.random.permutation(np.resize(levels, k // 32))).repeat(32)
    a = np.empty((k // 512, 16))
    for p in range(k // 512):
        a[p, :8] = np.random.permutation(np.resize(levels, 8))
        for g in range(8):
            far = levels[np.abs(levels - a[p, g]) >= 10]
            a[p, g + 8] = far[np.random.randint(len(far))]
    return np.exp2(a.ravel()).repeat(32)


def f64(x):
    return np.asarray(x).astype(np.float64)


def striped(idx):
    return np.tile(np.asarray(idx).reshape(-1, 16).T, (8, 1)).astype(np.uint16)


def unstriped(offs):
    return offs[:16].T.reshape(-1).astype(np.int64)


def striped8(idx):
    return np.asarray(idx).reshape(8, -1, 16).transpose(0, 2, 1).reshape(128, -1).astype(np.uint16)


def unstriped8(offs):
    return offs.reshape(8, 16, -1).transpose(0, 2, 1).reshape(8, -1).astype(np.int64)


def pick8(x, idx, run):
    r = np.arange(len(x))
    return x[r[:, None], idx[r % (8 * run) // run]]


E2M1 = np.array([0.0, 0.5, 1.0, 1.5, 2.0, 3.0, 4.0, 6.0, -0.0, -0.5, -1.0, -1.5, -2.0, -3.0, -4.0, -6.0])


def pack_weight(w, fmt):
    k, n = w.shape
    w = f64(np.asarray(w, np.float32).astype(ml_dtypes.bfloat16)).reshape(k // 32, 32, n)
    amax = np.abs(w).max(1)
    if fmt == "e4m3":
        byte = np.frexp(amax)[1] - 1 + 127 - 7
    else:
        mant, ex = np.frexp(amax / 6.0)
        byte = np.where(mant > 0.5, ex, ex - 1) + 127
    byte = np.clip(np.where(amax > 0, byte, 1), 1, 254)
    scaled = (w * np.exp2(127.0 - byte)[:, None, :]).reshape(k, n).astype(np.float32)
    by_word = np.ascontiguousarray(scaled.reshape(k // 512, 128, 4, n).transpose(0, 1, 3, 2))
    if fmt == "e4m3":
        words = by_word.astype(ml_dtypes.float8_e4m3fn).view(np.uint8)
    else:
        c = by_word.astype(ml_dtypes.float4_e2m1fn).view(np.uint8) & 0xF
        words = (c[..., 0::2] | (c[..., 1::2] << 4)).reshape(k // 512, 128, 2 * n)
    return np.ascontiguousarray(words), np.ascontiguousarray(byte.astype(np.uint8).reshape(k // 512, 16, n))


def unpack_weight(words, scales, fmt):
    g, _, n = scales.shape
    words = np.ascontiguousarray(words).reshape(g, 128, n, -1)
    if fmt == "e4m3":
        vals = words.view(ml_dtypes.float8_e4m3fn).astype(np.float64)
    else:
        nib = np.empty((g, 128, n, 4), np.uint8)
        nib[..., 0::2] = words & 0xF
        nib[..., 1::2] = words >> 4
        vals = E2M1[nib]
    vals = vals * np.repeat(np.exp2(scales.astype(np.float64) - 127.0), 8, axis=1)[..., None]
    return vals.transpose(0, 1, 3, 2).reshape(g * 512, n)


K, J, R, T, F, O, C, S, N, Z = 512, 512, 512, 2048, 1024, 256, 512, 256, 256, 1024


def setup_inputs():
    n = np.random.standard_normal
    idx = np.stack([np.random.permutation(T)[:J] for _ in range(8)])
    idx2 = np.random.permutation(F)[:R]
    idx3 = np.stack([np.random.permutation(J)[:S] for _ in range(8)])
    idx4 = np.stack([np.random.permutation(C)[:S] for _ in range(8)])
    idx5 = np.stack([np.random.permutation(C)[:O] for _ in range(8)])
    idx6 = np.stack([np.random.permutation(Z)[:N] for _ in range(8)])
    idx7 = np.stack([np.random.permutation(Z)[:N] for _ in range(8)])
    fk = mx_kscale(K)
    fr = mx_kscale(R)
    tr = np.ones(F)
    tr[idx2] = fr
    wtp = pack_weight(n((K, F)) * 1 / np.sqrt(K) / fk[:, None] * tr, "e2m1")
    return {
        "ta": (np.random.randint(-7, 8, (K, T)).astype(np.float64)).astype(np.float32),
        "ga": ((np.random.randint(8, 25, (K, 1)) / 64.0) * fk[:, None]).astype(np.float32),
        "wt_words": wtp[0],
        "wt_scales": wtp[1],
        "sa": (np.random.uniform(0.5, 1.6, (R, 1))).astype(np.float32),
        "sb": (np.random.uniform(0.5, 1.6, (R, 1))).astype(np.float32),
        "va": (np.random.randint(-7, 8, (R, Z)).astype(np.float64)).astype(np.float32),
        "ea": ((np.random.randint(10, 25, (R, 1)) / 1024.0) / fr[:, None]).astype(np.float32),
        "eb": ((np.random.randint(4, 13, (R, 1)) / 1024.0) / fr[:, None]).astype(np.float32),
        "offs": striped8(idx),
        "offs2": striped(idx2),
        "offs3": striped8(idx3),
        "offs4": striped8(idx4),
        "offs5": striped8(idx5),
        "offs6": striped8(idx6),
        "offs7": striped8(idx7),
    }


def reference(ta, ga, wt_words, wt_scales, sa, sb, va, ea, eb, offs, offs2, offs3, offs4, offs5, offs6, offs7):
    idx = unstriped8(offs)
    idx2 = unstriped(offs2)
    idx3 = unstriped8(offs3)
    idx4 = unstriped8(offs4)
    idx5 = unstriped8(offs5)
    idx6 = unstriped8(offs6)
    idx7 = unstriped8(offs7)
    wtu = unpack_weight(wt_words, wt_scales, "e2m1")
    xc = pick8(f64(ta), idx, 64) * f64(ga)
    wtidx2g = wtu[:, idx2]
    xcq = mxq(xc, 0, "e4m3")
    a = wtidx2g.T @ xcq
    h1 = pick8(a, idx3, 64) * f64(sa)
    pw = np.zeros((R, C))
    pw[np.arange(R)[:, None], idx4[np.arange(R) % 512 // 64]] = h1
    g1 = np.maximum(pw, 0.0)
    hid = pick8(g1, idx5, 64) * f64(sb)
    vc = pick8(f64(va), idx6, 64) * f64(ea) + pick8(f64(va), idx7, 64) * f64(eb)
    vcq = mxq(vc, 0, "e4m3")
    hidq = mxq(hid, 0, "e4m3")
    y = vcq.T @ hidq
    return y

@@ -1,0 +1,222 @@
+from contextlib import ExitStack
+
+import concourse.mybir as mybir
+
+K, J, R, T, F, O, C, S, N, Z = 512, 512, 512, 2048, 1024, 256, 512, 256, 256, 1024
+
+FLOPS = 2 * K * R * J + 2 * R * N * O
+
+F32 = mybir.dt.float32
+BF16 = mybir.dt.bfloat16
+I32 = mybir.dt.int32
+U32 = mybir.dt.uint32
+U16 = mybir.dt.uint16
+U8 = mybir.dt.uint8
+FP8X4 = mybir.dt.float8_e4m3fn_x4
+FP4X4 = mybir.dt.float4_e2m1fn_x4
+ACT = mybir.ActivationFunctionType
+ALU = mybir.AluOpType
+
+P = 128
+PACK = 4
+
+
+def tile_picked_codes_store_one_weighedposting_refined_plain_kernel(
+    tc, ta, ga, wt_words, wt_scales, sa, sb, va, ea, eb, offs, offs2, offs3, offs4, offs5, offs6, offs7, out
+):
+    nc = tc.nc
+    with ExitStack() as ctx:
+        lists = ctx.enter_context(tc.tile_pool(name="lists", bufs=1))
+        keep = ctx.enter_context(tc.tile_pool(name="keep", bufs=1))
+        psum = ctx.enter_context(tc.psum_pool(name="psum", bufs=1))
+
+        def load_list(src, name):
+            tile = lists.tile(list(src.shape), U16, name=name)
+            nc.sync.dma_start(tile[:], src)
+            return tile
+
+        def load_rows(queue, src, name):
+            tile = keep.tile([P, PACK], F32, name=name)
+            queue.dma_start(tile[:], src.rearrange("(p t) one -> p (t one)", t=PACK))
+            return tile
+
+        def load_plane(src, t, name):
+            tile = keep.tile([P, src.shape[1]], F32, name=name, tag=name)
+            nc.sync.dma_start(tile[:], src.rearrange("(p t) c -> p t c", t=PACK)[:, t, :])
+            return tile
+
+        ta_sb = [load_plane(ta, 0, "ta0")]
+        slot_list = load_list(offs, "slot_list")
+        ga_sb = load_rows(nc.scalar, ga, "ga_sb")
+        store_scales = keep.tile([P, F], U8, name="store_scales")
+        nc.vector.memset(store_scales[:].bitcast(I32), 0)
+        ta_sb.append(load_plane(ta, 1, "ta1"))
+        for q in range(4):
+            nc.sync.dma_start(
+                store_scales[32 * q : 32 * q + 4, :].bitcast(I32), wt_scales[0, 4 * q : 4 * q + 4, :].bitcast(I32)
+            )
+        store_list = load_list(offs2, "store_list")
+        store_words = keep.tile([P, F], U16, name="store_words")
+        nc.sync.dma_start(store_words[:].bitcast(I32), wt_words[0].bitcast(I32))
+        ta_sb.append(load_plane(ta, 2, "ta2"))
+        ta_sb.append(load_plane(ta, 3, "ta3"))
+        ea_sb = load_rows(nc.gpsimd, ea, "ea_sb")
+        eb_sb = load_rows(nc.gpsimd, eb, "eb_sb")
+        sa_sb = load_rows(nc.gpsimd, sa, "sa_sb")
+        sb_sb = load_rows(nc.gpsimd, sb, "sb_sb")
+        coarse_list = load_list(offs6, "coarse_list")
+        fine_list = load_list(offs7, "fine_list")
+        va_sb = [load_plane(va, 0, "va0")]
+        seat_list = load_list(offs3, "seat_list")
+        va_sb.append(load_plane(va, 1, "va1"))
+        board_list = load_list(offs4, "board_list")
+        place_list = load_list(offs5, "place_list")
+        va_sb.append(load_plane(va, 2, "va2"))
+        va_sb.append(load_plane(va, 3, "va3"))
+
+        board = [keep.tile([P, C], F32, name="board%d" % t) for t in range(PACK)]
+        for t in range(PACK):
+            nc.vector.memset(board[t][:], 0.0)
+
+        picked_words = keep.tile([P, R], U16, name="picked_words")
+        picked_scales = keep.tile([P, R], U8, name="picked_scales")
+        nc.vector.tensor_copy(picked_words[:], store_words[:].indirect(store_list[:]))
+        nc.vector.tensor_copy(picked_scales[:], store_scales[:].indirect(store_list[:]))
+        w_words = [
+            keep.tile([P, 2 * 2 * P], U8, name="w_words%d" % u, tag="w_words%d" % u, align_bytes=64) for u in range(2)
+        ]
+        w_scales = keep.tile([P, R], U8, name="w_scales", align_bytes=64)
+        for u in range(2):
+            nc.vector.tensor_copy(
+                w_words[u][:].rearrange("p (t m b) -> p t m b", t=2, b=2),
+                picked_words[:].bitcast(U8).rearrange("p (m t b) -> p t m b", t=PACK, b=2)[:, 2 * u : 2 * u + 2],
+            )
+        nc.vector.tensor_copy(
+            w_scales[:].rearrange("p (t m) -> p t m", t=PACK),
+            picked_scales[:].rearrange("p (m t) -> p t m", t=PACK),
+        )
+
+        xc_pair = [keep.tile([P, 2, J], BF16, name="xc_pair%d" % u) for u in range(2)]
+        xc_woven = keep.tile([P, J, PACK], BF16, name="xc_woven", align_bytes=64)
+        xc_codes = keep.tile([P, J], U32, name="xc_codes", align_bytes=64)
+        xc_scales = keep.tile([P, J], U8, name="xc_scales", align_bytes=64)
+        for t in range(PACK):
+            nc.scalar.activation(
+                out=xc_pair[t // 2][:, t % 2, :],
+                in_=ta_sb[t][:].indirect(slot_list[:]),
+                func=ACT.Copy,
+                scale=ga_sb[:, t : t + 1],
+            )
+        halves = [slice(0, J // 2), slice(J // 2, J)]
+        nc.vector.tensor_copy(xc_woven[:, :, 0:2], xc_pair[0][:].rearrange("p t j -> p j t"))
+        for js in halves:
+            nc.vector.tensor_copy(xc_woven[:, js, 2:4], xc_pair[1][:, :, js].rearrange("p t j -> p j t"))
+        for js in halves:
+            nc.vector.quantize_mx(
+                out=xc_codes[:, js].bitcast(FP8X4),
+                scales=xc_scales[:, js],
+                in_=xc_woven[:, js, :].rearrange("p j t -> p (j t)"),
+            )
+
+        def first_product(t, js, name):
+            acc = psum.tile([P, js.stop - js.start], F32, name=name)
+            nc.tensor.matmul_mx(
+                out=acc[:],
+                lhsT=w_words[t // 2][:, 2 * P * (t % 2) : 2 * P * (t % 2 + 1)].bitcast(FP4X4),
+                lhsT_scale=w_scales[:, P * t : P * (t + 1)],
+                rhs=xc_codes[:, js].bitcast(FP8X4),
+                rhs_scale=xc_scales[:, js],
+                start=True,
+                stop=True,
+            )
+            return acc
+
+        h1 = [keep.tile([P, S], F32, name="h1_%d" % t) for t in range(PACK)]
+        kept = [keep.tile([P, S], F32, name="kept%d" % t, tag="kept%d" % t, align_bytes=64) for t in range(PACK)]
+        a_sb = []
+        for t in range(PACK):
+            a_sb.append(keep.tile([P, J], F32, name="a%d" % t, tag="a%d" % (t % 2)))
+            if t == 0:
+                for u, js in enumerate(halves):
+                    acc = first_product(t, js, "a_acc0_%d" % u)
+                    nc.vector.tensor_copy(a_sb[t][:, js], acc[:])
+            else:
+                acc = first_product(t, slice(0, J), "a_acc%d" % t)
+                if t == 1:
+                    nc.vector.tensor_copy(a_sb[t][:], acc[:])
+                else:
+                    nc.scalar.copy(a_sb[t][:], acc[:])
+            nc.scalar.activation(
+                out=h1[t][:], in_=a_sb[t][:].indirect(seat_list[:]), func=ACT.Copy, scale=sa_sb[:, t : t + 1]
+            )
+            nc.scalar.activation(out=kept[t][:], in_=h1[t][:], func=ACT.Relu)
+            nc.vector.tensor_copy(board[t][:].indirect(board_list[:]), kept[t][:])
+
+        coarse = [keep.tile([P, 2, N], F32, name="coarse0"), keep.tile([P, 2, N], F32, name="coarse1", tag="a0")]
+        fine = [keep.tile([P, 2, N], F32, name="fine0"), keep.tile([P, 2, N], F32, name="fine1", tag="a1")]
+        vc_woven = keep.tile([P, N, PACK], BF16, name="vc_woven", tag="w_words0", align_bytes=64)
+        for t in range(PACK):
+            nc.scalar.activation(
+                out=coarse[t // 2][:, t % 2, :],
+                in_=va_sb[t][:].indirect(coarse_list[:]),
+                func=ACT.Copy,
+                scale=ea_sb[:, t : t + 1],
+            )
+            nc.scalar.activation(
+                out=fine[t // 2][:, t % 2, :],
+                in_=va_sb[t][:].indirect(fine_list[:]),
+                func=ACT.Copy,
+                scale=eb_sb[:, t : t + 1],
+            )
+            if t % 2 == 1:
+                u = t // 2
+                nc.vector.tensor_tensor(
+                    vc_woven[:, :, 2 * u : 2 * u + 2],
+                    coarse[u][:].rearrange("p t n -> p n t"),
+                    fine[u][:].rearrange("p t n -> p n t"),
+                    ALU.add,
+                )
+
+        hid_pair = [keep.tile([P, 2, O], BF16, name="hid_pair%d" % u, tag="va%d" % (3 - u)) for u in range(2)]
+        hid_woven = keep.tile([P, O, PACK], BF16, name="hid_woven", tag="kept3", align_bytes=64)
+        for t in range(PACK):
+            nc.scalar.activation(
+                out=hid_pair[t // 2][:, t % 2, :],
+                in_=board[t][:].indirect(place_list[:]),
+                func=ACT.Copy,
+                scale=sb_sb[:, t : t + 1],
+            )
+            if t % 2 == 1:
+                u = t // 2
+                nc.vector.tensor_copy(hid_woven[:, :, 2 * u : 2 * u + 2], hid_pair[u][:].rearrange("p t o -> p o t"))
+
+        vc_codes = keep.tile([P, N], U32, name="vc_codes", align_bytes=64)
+        vc_scales = keep.tile([P, N], U8, name="vc_scales", align_bytes=64)
+        hid_codes = keep.tile([P, O], U32, name="hid_codes", align_bytes=64)
+        hid_scales = keep.tile([P, O], U8, name="hid_scales", align_bytes=64)
+        nc.vector.quantize_mx(
+            out=vc_codes[:].bitcast(FP8X4), scales=vc_scales[:], in_=vc_woven[:].rearrange("p n t -> p (n t)")
+        )
+        nc.vector.quantize_mx(
+            out=hid_codes[:].bitcast(FP8X4), scales=hid_scales[:], in_=hid_woven[:].rearrange("p o t -> p (o t)")
+        )
+
+        for u in range(N // P):
+            ns = slice(u * P, (u + 1) * P)
+            acc = psum.tile([P, O], F32, name="y_acc%d" % u)
+            nc.tensor.matmul_mx(
+                out=acc[:],
+                lhsT=vc_codes[:, ns].bitcast(FP8X4),
+                lhsT_scale=vc_scales[:, ns],
+                rhs=hid_codes[:].bitcast(FP8X4),
+                rhs_scale=hid_scales[:],
+                start=True,
+                stop=True,
+            )
+            y_sb = keep.tile([P, O], F32, name="y_sb%d" % u)
+            if u == 0:
+                nc.vector.tensor_copy(y_sb[:], acc[:])
+                nc.sync.dma_start(out[ns, :], y_sb[:])
+            else:
+                nc.scalar.copy(y_sb[:], acc[:])
+                nc.scalar.dma_start(out[ns, :], y_sb[:])

@@ -28,6 +28,7 @@ def tile_picked_codes_store_one_weighedposting_refined_plain_kernel(
     with ExitStack() as ctx:
         lists = ctx.enter_context(tc.tile_pool(name="lists", bufs=1))
         keep = ctx.enter_context(tc.tile_pool(name="keep", bufs=1))
+        relay = ctx.enter_context(tc.tile_pool(name="relay", bufs=1))
         psum = ctx.enter_context(tc.psum_pool(name="psum", bufs=1))
 
         def load_list(src, name):
@@ -66,13 +67,12 @@ def tile_picked_codes_store_one_weighedposting_refined_plain_kernel(
         sb_sb = load_rows(nc.gpsimd, sb, "sb_sb")
         coarse_list = load_list(offs6, "coarse_list")
         fine_list = load_list(offs7, "fine_list")
-        va_sb = [load_plane(va, 0, "va0")]
+        va_sb = [load_plane(va, 0, "va0"), load_plane(va, 1, "va1")]
         seat_list = load_list(offs3, "seat_list")
-        va_sb.append(load_plane(va, 1, "va1"))
         board_list = load_list(offs4, "board_list")
-        place_list = load_list(offs5, "place_list")
         va_sb.append(load_plane(va, 2, "va2"))
         va_sb.append(load_plane(va, 3, "va3"))
+        place_list = load_list(offs5, "place_list")
 
         board = [keep.tile([P, C], F32, name="board%d" % t) for t in range(PACK)]
         for t in range(PACK):
@@ -97,7 +97,7 @@ def tile_picked_codes_store_one_weighedposting_refined_plain_kernel(
         )
 
         xc_pair = [keep.tile([P, 2, J], BF16, name="xc_pair%d" % u) for u in range(2)]
-        xc_woven = keep.tile([P, J, PACK], BF16, name="xc_woven", align_bytes=64)
+        xc_woven = keep.tile([P, J, PACK], BF16, name="xc_woven", tag="xc_woven", align_bytes=64)
         xc_codes = keep.tile([P, J], U32, name="xc_codes", align_bytes=64)
         xc_scales = keep.tile([P, J], U8, name="xc_scales", align_bytes=64)
         for t in range(PACK):
@@ -131,92 +131,111 @@ def tile_picked_codes_store_one_weighedposting_refined_plain_kernel(
             )
             return acc
 
-        h1 = [keep.tile([P, S], F32, name="h1_%d" % t) for t in range(PACK)]
-        kept = [keep.tile([P, S], F32, name="kept%d" % t, tag="kept%d" % t, align_bytes=64) for t in range(PACK)]
-        a_sb = []
-        for t in range(PACK):
-            a_sb.append(keep.tile([P, J], F32, name="a%d" % t, tag="a%d" % (t % 2)))
-            if t == 0:
-                for u, js in enumerate(halves):
-                    acc = first_product(t, js, "a_acc0_%d" % u)
-                    nc.vector.tensor_copy(a_sb[t][:, js], acc[:])
-            else:
-                acc = first_product(t, slice(0, J), "a_acc%d" % t)
-                if t == 1:
-                    nc.vector.tensor_copy(a_sb[t][:], acc[:])
-                else:
-                    nc.scalar.copy(a_sb[t][:], acc[:])
-            nc.scalar.activation(
-                out=h1[t][:], in_=a_sb[t][:].indirect(seat_list[:]), func=ACT.Copy, scale=sa_sb[:, t : t + 1]
-            )
-            nc.scalar.activation(out=kept[t][:], in_=h1[t][:], func=ACT.Relu)
-            nc.vector.tensor_copy(board[t][:].indirect(board_list[:]), kept[t][:])
+        vc_planes = keep.tile([P, PACK, N], BF16, name="vc_planes", tag="xc_woven", align_bytes=64)
 
-        coarse = [keep.tile([P, 2, N], F32, name="coarse0"), keep.tile([P, 2, N], F32, name="coarse1", tag="a0")]
-        fine = [keep.tile([P, 2, N], F32, name="fine0"), keep.tile([P, 2, N], F32, name="fine1", tag="a1")]
-        vc_woven = keep.tile([P, N, PACK], BF16, name="vc_woven", tag="w_words0", align_bytes=64)
-        for t in range(PACK):
+        def output_terms(t, coarse, fine):
             nc.scalar.activation(
-                out=coarse[t // 2][:, t % 2, :],
+                out=coarse,
                 in_=va_sb[t][:].indirect(coarse_list[:]),
                 func=ACT.Copy,
                 scale=ea_sb[:, t : t + 1],
             )
             nc.scalar.activation(
-                out=fine[t // 2][:, t % 2, :],
+                out=fine,
                 in_=va_sb[t][:].indirect(fine_list[:]),
                 func=ACT.Copy,
                 scale=eb_sb[:, t : t + 1],
             )
-            if t % 2 == 1:
-                u = t // 2
-                nc.vector.tensor_tensor(
-                    vc_woven[:, :, 2 * u : 2 * u + 2],
-                    coarse[u][:].rearrange("p t n -> p n t"),
-                    fine[u][:].rearrange("p t n -> p n t"),
-                    ALU.add,
-                )
+            nc.gpsimd.tensor_tensor(vc_planes[:, t, :], coarse, fine, ALU.add)
 
-        hid_pair = [keep.tile([P, 2, O], BF16, name="hid_pair%d" % u, tag="va%d" % (3 - u)) for u in range(2)]
-        hid_woven = keep.tile([P, O, PACK], BF16, name="hid_woven", tag="kept3", align_bytes=64)
+        early_terms = keep.tile([P, 4, N], F32, name="early_terms")
+        for t in range(2):
+            output_terms(t, early_terms[:, 2 * t, :], early_terms[:, 2 * t + 1, :])
+        h1_first = keep.tile([P, S], F32, name="h1_first", tag="va1")
+        kept_first = keep.tile([P, S], F32, name="kept_first")
+        kept_mid = keep.tile([P, 2, S], F32, name="kept_mid")
+        kept_last = keep.tile([P, S], F32, name="kept_last", tag="kept_last", align_bytes=64)
+        kept = [kept_first[:], kept_mid[:, 0, :], kept_mid[:, 1, :], kept_last[:]]
+
+        def seats(t, a_sb, h1):
+            if t == 0:
+                for u, js in enumerate(halves):
+                    nc.vector.tensor_copy(a_sb[:, js], first_product(t, js, "a_acc0_%d" % u)[:])
+            elif t < 3:
+                nc.vector.tensor_copy(a_sb[:], first_product(t, slice(0, J), "a_acc%d" % t)[:])
+            else:
+                nc.scalar.copy(a_sb[:], first_product(t, slice(0, J), "a_acc%d" % t)[:])
+            nc.scalar.activation(
+                out=h1, in_=a_sb[:].indirect(seat_list[:]), func=ACT.Copy, scale=sa_sb[:, t : t + 1]
+            )
+
+        def post(t):
+            nc.vector.tensor_copy(board[t][:].indirect(board_list[:]), kept[t])
+
+        seats(0, keep.tile([P, J], F32, name="a0", tag="a0"), h1_first[:])
+        h1_mid = keep.tile([P, 2, S], F32, name="h1_mid", tag="a0")
+        h1_last = keep.tile([P, S], F32, name="h1_last")
+        seats(1, keep.tile([P, J], F32, name="a1"), h1_mid[:, 0, :])
+        seats(2, relay.tile([P, J], F32, name="a2", offset=3072), h1_mid[:, 1, :])
+        nc.vector.tensor_scalar_max(kept[0], h1_first[:], 0.0)
+        post(0)
+        nc.scalar.activation(out=kept[1], in_=h1_mid[:, 0, :], func=ACT.Relu)
+        post(1)
+        nc.gpsimd.tensor_scalar_max(kept[2], h1_mid[:, 1, :], 0.0)
+        post(2)
+        seats(3, relay.tile([P, J], F32, name="a3", offset=4096), h1_last[:])
+        nc.gpsimd.tensor_scalar_max(kept[3], h1_last[:], 0.0)
+        post(3)
+
+        late_terms = relay.tile([P, 4, N], F32, name="late_terms", offset=0)
+        for t in range(2):
+            output_terms(2 + t, late_terms[:, 2 * t, :], late_terms[:, 2 * t + 1, :])
+
+        hid_planes = keep.tile([P, PACK, O], BF16, name="hid_planes", tag="va3")
         for t in range(PACK):
             nc.scalar.activation(
-                out=hid_pair[t // 2][:, t % 2, :],
+                out=hid_planes[:, t, :],
                 in_=board[t][:].indirect(place_list[:]),
                 func=ACT.Copy,
                 scale=sb_sb[:, t : t + 1],
             )
-            if t % 2 == 1:
-                u = t // 2
-                nc.vector.tensor_copy(hid_woven[:, :, 2 * u : 2 * u + 2], hid_pair[u][:].rearrange("p t o -> p o t"))
+        def weave(copy, woven, planes):
+            copy(woven.rearrange("p (c i) t -> p c t i", i=4), planes.rearrange("p t (c i) -> p c t i", i=4))
 
-        vc_codes = keep.tile([P, N], U32, name="vc_codes", align_bytes=64)
-        vc_scales = keep.tile([P, N], U8, name="vc_scales", align_bytes=64)
-        hid_codes = keep.tile([P, O], U32, name="hid_codes", align_bytes=64)
-        hid_scales = keep.tile([P, O], U8, name="hid_scales", align_bytes=64)
-        nc.vector.quantize_mx(
-            out=vc_codes[:].bitcast(FP8X4), scales=vc_scales[:], in_=vc_woven[:].rearrange("p n t -> p (n t)")
-        )
-        nc.vector.quantize_mx(
-            out=hid_codes[:].bitcast(FP8X4), scales=hid_scales[:], in_=hid_woven[:].rearrange("p o t -> p (o t)")
-        )
-
-        for u in range(N // P):
-            ns = slice(u * P, (u + 1) * P)
-            acc = psum.tile([P, O], F32, name="y_acc%d" % u)
-            nc.tensor.matmul_mx(
-                out=acc[:],
-                lhsT=vc_codes[:, ns].bitcast(FP8X4),
-                lhsT_scale=vc_scales[:, ns],
-                rhs=hid_codes[:].bitcast(FP8X4),
-                rhs_scale=hid_scales[:],
-                start=True,
-                stop=True,
+        def quantize(woven, name):
+            codes = keep.tile([P, woven.shape[1]], U32, name=name + "_codes", align_bytes=64)
+            scales = keep.tile([P, woven.shape[1]], U8, name=name + "_scales", align_bytes=64)
+            nc.vector.quantize_mx(
+                out=codes[:].bitcast(FP8X4), scales=scales[:], in_=woven[:].rearrange("p c t -> p (c t)")
             )
-            y_sb = keep.tile([P, O], F32, name="y_sb%d" % u)
-            if u == 0:
-                nc.vector.tensor_copy(y_sb[:], acc[:])
-                nc.sync.dma_start(out[ns, :], y_sb[:])
-            else:
+            return codes, scales
+
+        vc_woven = keep.tile([P, N, PACK], BF16, name="vc_woven", tag="kept_last", align_bytes=64)
+        weave(nc.vector.tensor_copy, vc_woven[:], vc_planes[:])
+        hid_woven = [keep.tile([P, O // 2, PACK], BF16, name="hid_woven%d" % v, align_bytes=64) for v in range(2)]
+        weave(nc.vector.tensor_copy, hid_woven[0][:], hid_planes[:, :, 0 : O // 2])
+        weave(nc.scalar.copy, hid_woven[1][:], hid_planes[:, :, O // 2 : O])
+        vc_codes, vc_scales = quantize(vc_woven, "vc")
+
+        for v in range(2):
+            hid_codes, hid_scales = quantize(hid_woven[v], "hid%d" % v)
+            acc = psum.tile([P, N // P, O // 2], F32, name="y_acc%d" % v)
+            for u in range(N // P):
+                ns = slice(u * P, (u + 1) * P)
+                nc.tensor.matmul_mx(
+                    out=acc[:, u, :],
+                    lhsT=vc_codes[:, ns].bitcast(FP8X4),
+                    lhsT_scale=vc_scales[:, ns],
+                    rhs=hid_codes[:].bitcast(FP8X4),
+                    rhs_scale=hid_scales[:],
+                    start=True,
+                    stop=True,
+                )
+            y_sb = keep.tile([P, N // P, O // 2], F32, name="y_sb%d" % v)
+            y_out = out.rearrange("(u p) o -> p u o", p=P)[:, :, v * (O // 2) : (v + 1) * (O // 2)]
+            if v == 0:
                 nc.scalar.copy(y_sb[:], acc[:])
-                nc.scalar.dma_start(out[ns, :], y_sb[:])
+                nc.scalar.dma_start(y_out, y_sb[:])
+            else:
+                nc.vector.tensor_copy(y_sb[:], acc[:])
+                nc.sync.dma_start(y_out, y_sb[:])

from contextlib import ExitStack

import concourse.mybir as mybir

K, J, R, T, F, O, C, S, N, Z = 512, 512, 512, 2048, 1024, 256, 512, 256, 256, 1024

FLOPS = 2 * K * R * J + 2 * R * N * O

F32 = mybir.dt.float32
BF16 = mybir.dt.bfloat16
I32 = mybir.dt.int32
U32 = mybir.dt.uint32
U16 = mybir.dt.uint16
U8 = mybir.dt.uint8
FP8X4 = mybir.dt.float8_e4m3fn_x4
FP4X4 = mybir.dt.float4_e2m1fn_x4
ACT = mybir.ActivationFunctionType
ALU = mybir.AluOpType

P = 128
PACK = 4


def tile_picked_codes_store_one_weighedposting_refined_plain_kernel(
    tc, ta, ga, wt_words, wt_scales, sa, sb, va, ea, eb, offs, offs2, offs3, offs4, offs5, offs6, offs7, out
):
    nc = tc.nc
    with ExitStack() as ctx:
        lists = ctx.enter_context(tc.tile_pool(name="lists", bufs=1))
        keep = ctx.enter_context(tc.tile_pool(name="keep", bufs=1))
        relay = ctx.enter_context(tc.tile_pool(name="relay", bufs=1))
        psum = ctx.enter_context(tc.psum_pool(name="psum", bufs=1))

        def load_list(src, name):
            tile = lists.tile(list(src.shape), U16, name=name)
            nc.sync.dma_start(tile[:], src)
            return tile

        def load_rows(queue, src, name):
            tile = keep.tile([P, PACK], F32, name=name)
            queue.dma_start(tile[:], src.rearrange("(p t) one -> p (t one)", t=PACK))
            return tile

        def load_plane(src, t, name):
            tile = keep.tile([P, src.shape[1]], F32, name=name, tag=name)
            nc.sync.dma_start(tile[:], src.rearrange("(p t) c -> p t c", t=PACK)[:, t, :])
            return tile

        ta_sb = [load_plane(ta, 0, "ta0")]
        slot_list = load_list(offs, "slot_list")
        ga_sb = load_rows(nc.scalar, ga, "ga_sb")
        store_scales = keep.tile([P, F], U8, name="store_scales")
        nc.vector.memset(store_scales[:].bitcast(I32), 0)
        ta_sb.append(load_plane(ta, 1, "ta1"))
        for q in range(4):
            nc.sync.dma_start(
                store_scales[32 * q : 32 * q + 4, :].bitcast(I32), wt_scales[0, 4 * q : 4 * q + 4, :].bitcast(I32)
            )
        store_list = load_list(offs2, "store_list")
        store_words = keep.tile([P, F], U16, name="store_words")
        nc.sync.dma_start(store_words[:].bitcast(I32), wt_words[0].bitcast(I32))
        ta_sb.append(load_plane(ta, 2, "ta2"))
        ta_sb.append(load_plane(ta, 3, "ta3"))
        ea_sb = load_rows(nc.gpsimd, ea, "ea_sb")
        eb_sb = load_rows(nc.gpsimd, eb, "eb_sb")
        sa_sb = load_rows(nc.gpsimd, sa, "sa_sb")
        sb_sb = load_rows(nc.gpsimd, sb, "sb_sb")
        coarse_list = load_list(offs6, "coarse_list")
        fine_list = load_list(offs7, "fine_list")
        va_sb = [load_plane(va, 0, "va0"), load_plane(va, 1, "va1")]
        seat_list = load_list(offs3, "seat_list")
        board_list = load_list(offs4, "board_list")
        va_sb.append(load_plane(va, 2, "va2"))
        va_sb.append(load_plane(va, 3, "va3"))
        place_list = load_list(offs5, "place_list")

        board = [keep.tile([P, C], F32, name="board%d" % t) for t in range(PACK)]
        for t in range(PACK):
            nc.vector.memset(board[t][:], 0.0)

        picked_words = keep.tile([P, R], U16, name="picked_words")
        picked_scales = keep.tile([P, R], U8, name="picked_scales")
        nc.vector.tensor_copy(picked_words[:], store_words[:].indirect(store_list[:]))
        nc.vector.tensor_copy(picked_scales[:], store_scales[:].indirect(store_list[:]))
        w_words = [
            keep.tile([P, 2 * 2 * P], U8, name="w_words%d" % u, tag="w_words%d" % u, align_bytes=64) for u in range(2)
        ]
        w_scales = keep.tile([P, R], U8, name="w_scales", align_bytes=64)
        for u in range(2):
            nc.vector.tensor_copy(
                w_words[u][:].rearrange("p (t m b) -> p t m b", t=2, b=2),
                picked_words[:].bitcast(U8).rearrange("p (m t b) -> p t m b", t=PACK, b=2)[:, 2 * u : 2 * u + 2],
            )
        nc.vector.tensor_copy(
            w_scales[:].rearrange("p (t m) -> p t m", t=PACK),
            picked_scales[:].rearrange("p (m t) -> p t m", t=PACK),
        )

        xc_pair = [keep.tile([P, 2, J], BF16, name="xc_pair%d" % u) for u in range(2)]
        xc_woven = keep.tile([P, J, PACK], BF16, name="xc_woven", tag="xc_woven", align_bytes=64)
        xc_codes = keep.tile([P, J], U32, name="xc_codes", align_bytes=64)
        xc_scales = keep.tile([P, J], U8, name="xc_scales", align_bytes=64)
        for t in range(PACK):
            nc.scalar.activation(
                out=xc_pair[t // 2][:, t % 2, :],
                in_=ta_sb[t][:].indirect(slot_list[:]),
                func=ACT.Copy,
                scale=ga_sb[:, t : t + 1],
            )
        halves = [slice(0, J // 2), slice(J // 2, J)]
        nc.vector.tensor_copy(xc_woven[:, :, 0:2], xc_pair[0][:].rearrange("p t j -> p j t"))
        for js in halves:
            nc.vector.tensor_copy(xc_woven[:, js, 2:4], xc_pair[1][:, :, js].rearrange("p t j -> p j t"))
        for js in halves:
            nc.vector.quantize_mx(
                out=xc_codes[:, js].bitcast(FP8X4),
                scales=xc_scales[:, js],
                in_=xc_woven[:, js, :].rearrange("p j t -> p (j t)"),
            )

        def first_product(t, js, name):
            acc = psum.tile([P, js.stop - js.start], F32, name=name)
            nc.tensor.matmul_mx(
                out=acc[:],
                lhsT=w_words[t // 2][:, 2 * P * (t % 2) : 2 * P * (t % 2 + 1)].bitcast(FP4X4),
                lhsT_scale=w_scales[:, P * t : P * (t + 1)],
                rhs=xc_codes[:, js].bitcast(FP8X4),
                rhs_scale=xc_scales[:, js],
                start=True,
                stop=True,
            )
            return acc

        vc_planes = keep.tile([P, PACK, N], BF16, name="vc_planes", tag="xc_woven", align_bytes=64)

        def output_terms(t, coarse, fine):
            nc.scalar.activation(
                out=coarse,
                in_=va_sb[t][:].indirect(coarse_list[:]),
                func=ACT.Copy,
                scale=ea_sb[:, t : t + 1],
            )
            nc.scalar.activation(
                out=fine,
                in_=va_sb[t][:].indirect(fine_list[:]),
                func=ACT.Copy,
                scale=eb_sb[:, t : t + 1],
            )
            nc.gpsimd.tensor_tensor(vc_planes[:, t, :], coarse, fine, ALU.add)

        early_terms = keep.tile([P, 4, N], F32, name="early_terms")
        for t in range(2):
            output_terms(t, early_terms[:, 2 * t, :], early_terms[:, 2 * t + 1, :])
        h1_first = keep.tile([P, S], F32, name="h1_first", tag="va1")
        kept_first = keep.tile([P, S], F32, name="kept_first")
        kept_mid = keep.tile([P, 2, S], F32, name="kept_mid")
        kept_last = keep.tile([P, S], F32, name="kept_last", tag="kept_last", align_bytes=64)
        kept = [kept_first[:], kept_mid[:, 0, :], kept_mid[:, 1, :], kept_last[:]]

        def seats(t, a_sb, h1):
            if t == 0:
                for u, js in enumerate(halves):
                    nc.vector.tensor_copy(a_sb[:, js], first_product(t, js, "a_acc0_%d" % u)[:])
            elif t < 3:
                nc.vector.tensor_copy(a_sb[:], first_product(t, slice(0, J), "a_acc%d" % t)[:])
            else:
                nc.scalar.copy(a_sb[:], first_product(t, slice(0, J), "a_acc%d" % t)[:])
            nc.scalar.activation(
                out=h1, in_=a_sb[:].indirect(seat_list[:]), func=ACT.Copy, scale=sa_sb[:, t : t + 1]
            )

        def post(t):
            nc.vector.tensor_copy(board[t][:].indirect(board_list[:]), kept[t])

        seats(0, keep.tile([P, J], F32, name="a0", tag="a0"), h1_first[:])
        h1_mid = keep.tile([P, 2, S], F32, name="h1_mid", tag="a0")
        h1_last = keep.tile([P, S], F32, name="h1_last")
        seats(1, keep.tile([P, J], F32, name="a1"), h1_mid[:, 0, :])
        seats(2, relay.tile([P, J], F32, name="a2", offset=3072), h1_mid[:, 1, :])
        nc.vector.tensor_scalar_max(kept[0], h1_first[:], 0.0)
        post(0)
        nc.scalar.activation(out=kept[1], in_=h1_mid[:, 0, :], func=ACT.Relu)
        post(1)
        nc.gpsimd.tensor_scalar_max(kept[2], h1_mid[:, 1, :], 0.0)
        post(2)
        seats(3, relay.tile([P, J], F32, name="a3", offset=4096), h1_last[:])
        nc.gpsimd.tensor_scalar_max(kept[3], h1_last[:], 0.0)
        post(3)

        late_terms = relay.tile([P, 4, N], F32, name="late_terms", offset=0)
        for t in range(2):
            output_terms(2 + t, late_terms[:, 2 * t, :], late_terms[:, 2 * t + 1, :])

        hid_planes = keep.tile([P, PACK, O], BF16, name="hid_planes", tag="va3")
        for t in range(PACK):
            nc.scalar.activation(
                out=hid_planes[:, t, :],
                in_=board[t][:].indirect(place_list[:]),
                func=ACT.Copy,
                scale=sb_sb[:, t : t + 1],
            )
        def weave(copy, woven, planes):
            copy(woven.rearrange("p (c i) t -> p c t i", i=4), planes.rearrange("p t (c i) -> p c t i", i=4))

        def quantize(woven, name):
            codes = keep.tile([P, woven.shape[1]], U32, name=name + "_codes", align_bytes=64)
            scales = keep.tile([P, woven.shape[1]], U8, name=name + "_scales", align_bytes=64)
            nc.vector.quantize_mx(
                out=codes[:].bitcast(FP8X4), scales=scales[:], in_=woven[:].rearrange("p c t -> p (c t)")
            )
            return codes, scales

        vc_woven = keep.tile([P, N, PACK], BF16, name="vc_woven", tag="kept_last", align_bytes=64)
        weave(nc.vector.tensor_copy, vc_woven[:], vc_planes[:])
        hid_woven = [keep.tile([P, O // 2, PACK], BF16, name="hid_woven%d" % v, align_bytes=64) for v in range(2)]
        weave(nc.vector.tensor_copy, hid_woven[0][:], hid_planes[:, :, 0 : O // 2])
        weave(nc.scalar.copy, hid_woven[1][:], hid_planes[:, :, O // 2 : O])
        vc_codes, vc_scales = quantize(vc_woven, "vc")

        for v in range(2):
            hid_codes, hid_scales = quantize(hid_woven[v], "hid%d" % v)
            acc = psum.tile([P, N // P, O // 2], F32, name="y_acc%d" % v)
            for u in range(N // P):
                ns = slice(u * P, (u + 1) * P)
                nc.tensor.matmul_mx(
                    out=acc[:, u, :],
                    lhsT=vc_codes[:, ns].bitcast(FP8X4),
                    lhsT_scale=vc_scales[:, ns],
                    rhs=hid_codes[:].bitcast(FP8X4),
                    rhs_scale=hid_scales[:],
                    start=True,
                    stop=True,
                )
            y_sb = keep.tile([P, N // P, O // 2], F32, name="y_sb%d" % v)
            y_out = out.rearrange("(u p) o -> p u o", p=P)[:, :, v * (O // 2) : (v + 1) * (O // 2)]
            if v == 0:
                nc.scalar.copy(y_sb[:], acc[:])
                nc.scalar.dma_start(y_out, y_sb[:])
            else:
                nc.vector.tensor_copy(y_sb[:], acc[:])
                nc.sync.dma_start(y_out, y_sb[:])
